import numpy as np
import ml_dtypes


def mxq(x, axis, fmt="e4m3"):
    dtype, down = {"e4m3": (ml_dtypes.float8_e4m3fn, 7), "e5m2": (ml_dtypes.float8_e5m2, 14)}[fmt]
    v = np.moveaxis(np.asarray(x, np.float32).astype(ml_dtypes.bfloat16).astype(np.float64), axis, -1)
    blocks = v.reshape(v.shape[:-1] + (-1, 32))
    amax = np.abs(blocks).max(-1, keepdims=True)
    byte = np.maximum(np.where(amax > 0, np.frexp(amax)[1] - 1 + 127, 0) - down, 1)
    scale = np.exp2(byte - 127.0)
    codes = (blocks / scale).astype(np.float32).astype(dtype).astype(np.float64)
    return np.moveaxis((codes * scale).reshape(v.shape), -1, axis)


WIDE = False


def mx_kscale(k):
    if not WIDE:
        return np.ones(k)
    levels = np.array([10, -10, 5, -5, 0])
    if k % 512:
        return np.exp2(np.random.permutation(np.resize(levels, k // 32))).repeat(32)
    a = np.empty((k // 512, 16))
    for p in range(k // 512):
        a[p, :8] = np.random.permutation(np.resize(levels, 8))
        for g in range(8):
            far = levels[np.abs(levels - a[p, g]) >= 10]
            a[p, g + 8] = far[np.random.randint(len(far))]
    return np.exp2(a.ravel()).repeat(32)


def f64(x):
    return np.asarray(x).astype(np.float64)


def striped(idx):
    return np.tile(idx.reshape(-1, 16).T, (8, 1)).astype(np.uint16)


def unstriped(offs):
    return offs[:16].T.reshape(-1).astype(np.int64)


def pack_weight(w):
    k, n = w.shape
    w = f64(np.asarray(w, np.float32).astype(ml_dtypes.bfloat16)).reshape(k // 32, 32, n)
    amax = np.abs(w).max(1)
    byte = np.clip(np.where(amax > 0, np.frexp(amax)[1] - 1 + 127 - 7, 1), 1, 254)
    scaled = (w * np.exp2(127.0 - byte)[:, None, :]).reshape(k, n).astype(np.float32)
    words = np.ascontiguousarray(scaled.reshape(k // 512, 128, 4, n).transpose(0, 1, 3, 2)).astype(ml_dtypes.float8_e4m3fn).view(np.uint8)
    return words, np.ascontiguousarray(byte.astype(np.uint8).reshape(k // 512, 16, n))


def unpack_weight(words, scales):
    g, p, n, _ = words.shape
    vals = np.ascontiguousarray(words).view(ml_dtypes.float8_e4m3fn).astype(np.float64) * np.repeat(np.exp2(scales.astype(np.float64) - 127.0), 8, axis=1)[..., None]
    return vals.transpose(0, 1, 3, 2).reshape(g * 512, n)


K, T, S, N, H, W, U = 512, 1024, 512, 128, 512, 1024, 1024


def setup_inputs():
    n = np.random.standard_normal
    s = mx_kscale(K)[:, None]
    u = mx_kscale(H)
    packed_xT = pack_weight(n((K, T)) * s)
    packed_eT = pack_weight(n((K, W)) * s)
    return {
        "x_words": packed_xT[0],
        "x_scales": packed_xT[1],
        "w1": (n((K, H)) / np.sqrt(K) / s).astype(np.float32),
        "e_words": packed_eT[0],
        "e_scales": packed_eT[1],
        "w2": (n((K, H)) / np.sqrt(K) / s).astype(np.float32),
        "imp": (np.random.uniform(0.3, 1.3, (H, U))).astype(np.float32),
        "unit": (np.random.uniform(0.6, 1.4, (H, 1)) * u[:, None]).astype(np.float32),
        "w3": (n((H, N)) / np.sqrt(H) / u[:, None]).astype(np.float32),
        "offs": striped(np.random.permutation(T)[:S]),
        "rem": striped(np.random.permutation(W)[:S]),
        "qu": striped(np.random.permutation(np.concatenate([np.arange(S), np.random.randint(0, S, U - S)]))),
        "re": striped(np.random.permutation(np.concatenate([np.arange(S), np.random.randint(0, S, U - S)]))),
        "hsh": striped(np.random.permutation(S)),
    }


def reference(x_words, x_scales, w1, e_words, e_scales, w2, imp, unit, w3, offs, rem, qu, re, hsh):
    xq = unpack_weight(x_words, x_scales)[:, unstriped(offs)]
    y = mxq(f64(w1), 0, "e4m3").T @ xq
    gq = y[:, unstriped(qu)]
    e_rem = unpack_weight(e_words, e_scales)[:, unstriped(rem)]
    ye = mxq(f64(w2), 0, "e4m3").T @ e_rem
    gr = ye[:, unstriped(re)]
    emb = gq * gr
    mixd = y[:, unstriped(hsh)] - ye
    emb2 = emb + f64(imp) * mixd[:, unstriped(re)]
    gt = np.exp(0.7 * np.tanh(emb))
    hid = f64(unit) * (emb2 * gt)
    return mxq(f64(w3), 0, "e4m3").T @ mxq(hid, 0, "e4m3")

@@ -1,0 +1,210 @@
+from contextlib import ExitStack
+
+import concourse.mybir as mybir
+from concourse.masks import make_identity
+
+K, T, S, N, H, U = 512, 1024, 512, 128, 512, 1024
+FLOPS = 2 * K * H * S * 2 + 2 * H * N * U
+
+F32 = mybir.dt.float32
+BF16 = mybir.dt.bfloat16
+I32 = mybir.dt.int32
+U32 = mybir.dt.uint32
+U16 = mybir.dt.uint16
+U8 = mybir.dt.uint8
+FP8X4 = mybir.dt.float8_e4m3fn_x4
+ACT = mybir.ActivationFunctionType
+ALU = mybir.AluOpType
+
+P = 128
+PACK = 4
+HALF = U // 2
+BLOCK = 128
+WIDE_WINDOW = 2 * S
+WINDOW = S + 16
+OUT_WIDTHS = (256, 256, 256, 128, 128)
+
+
+def tile_picked_yqrcmp_gate_p_kernel(
+    tc, x_words, x_scales, w1, e_words, e_scales, w2, imp, unit, w3, offs, rem, qu, re, hsh, out
+):
+    nc = tc.nc
+    with ExitStack() as ctx:
+        keep = ctx.enter_context(tc.tile_pool(name="keep", bufs=1))
+        psum = ctx.enter_context(tc.psum_pool(name="psum", bufs=1))
+
+        def sb(shape, dtype, name):
+            return keep.tile(shape, dtype, name=name, align_bytes=64)
+
+        def load_list(src, name):
+            buf = sb(list(src.shape), U16, name)
+            nc.sync.dma_start(buf[:], src)
+            return buf
+
+        def load_words(src, name):
+            buf = sb([P, T], U32, name)
+            nc.sync.dma_start(buf[:].bitcast(I32), src[0].rearrange("p n t -> p (n t)").bitcast(I32))
+            return buf
+
+        def load_scales(src, name, queue):
+            buf = sb([P, T], U8, name)
+            nc.vector.memset(buf[:].bitcast(I32), 0)
+            for q in range(4):
+                queue.dma_start(buf[32 * q : 32 * q + 4, :].bitcast(I32), src[0, 4 * q : 4 * q + 4, :].bitcast(I32))
+            return buf
+
+        def load_weight_half(w, half, name):
+            buf = sb([P, PACK, H // 2], F32, name)
+            cols = slice(half * (H // 2), (half + 1) * (H // 2))
+            nc.sync.dma_start(buf[:], w.rearrange("(p j) c -> p j c", j=PACK)[:, :, cols])
+            return buf
+
+        def window(width, name, engine):
+            buf = sb([P, width], F32, name)
+            engine.memset(buf[:, S:], 0.0)
+            return buf
+
+        offs_sb = load_list(offs, "offs_sb")
+        xw = load_words(x_words, "xw")
+        xs = load_scales(x_scales, "xs", nc.scalar)
+        es = load_scales(e_scales, "es", nc.gpsimd)
+        w1_raw = [load_weight_half(w1, 0, "w1_raw0")]
+        rem_sb = load_list(rem, "rem_sb")
+        w1_raw.append(load_weight_half(w1, 1, "w1_raw1"))
+        ew = load_words(e_words, "ew")
+        w2_raw = [load_weight_half(w2, half, "w2_raw%d" % half) for half in range(2)]
+        qu_sb = load_list(qu, "qu_sb")
+        hsh_sb = load_list(hsh, "hsh_sb")
+        re_sb = load_list(re, "re_sb")
+        unit_sb = sb([P, PACK], F32, "unit_sb")
+        nc.sync.dma_start(unit_sb[:], unit.rearrange("(p t) o -> p (t o)", t=PACK))
+        imp_sb = []
+        for h in range(2):
+            buf = sb([P, PACK, HALF], F32, "imp%d" % h)
+            nc.sync.dma_start(buf[:], imp.rearrange("(p t) r -> p t r", t=PACK)[:, :, h * HALF : (h + 1) * HALF])
+            imp_sb.append(buf)
+        w3_raw = sb([P, PACK, N], F32, "w3_raw")
+        nc.sync.dma_start(w3_raw[:], w3.rearrange("(p j) m -> p j m", j=PACK))
+
+        y_win = [window(WIDE_WINDOW, "y%d" % t, nc.vector) for t in range(PACK)]
+        ye_win = [window(WINDOW, "ye%d" % t, nc.gpsimd) for t in range(PACK)]
+        mix_win = [window(WINDOW, "mix%d" % t, nc.gpsimd) for t in range(PACK)]
+        ident = sb([P, P], F32, "ident")
+        make_identity(nc, ident[:])
+
+        def pick(table, offsets, dtype, name):
+            buf = sb([P, S], dtype, name)
+            nc.vector.tensor_copy(buf[:], table[:].indirect(offsets[:]))
+            return buf
+
+        def deal_weight(raw, name):
+            buf = sb([P, PACK, P, PACK], BF16, name)
+            for half in range(2):
+                nc.scalar.copy(
+                    buf[:, :, half * (P // 2) : (half + 1) * (P // 2), :].rearrange("p t m j -> p m j t"),
+                    raw[half][:].rearrange("p j (m t) -> p m j t", t=PACK),
+                )
+            return buf[:].rearrange("p t m j -> p (t m j)")
+
+        def quantize(values, width, name):
+            codes = sb([P, width], U32, name + "_codes")
+            scales = sb([P, width], U8, name + "_scales")
+            nc.vector.quantize_mx(out=codes[:].bitcast(FP8X4), scales=scales[:], in_=values)
+            return codes, scales
+
+        def product(bank, lhs, cols, rhs):
+            nc.tensor.matmul_mx(
+                out=bank,
+                lhsT=lhs[0][:, cols].bitcast(FP8X4),
+                lhsT_scale=lhs[1][:, cols],
+                rhs=rhs[0][:].bitcast(FP8X4),
+                rhs_scale=rhs[1][:],
+                start=True,
+                stop=True,
+            )
+
+        def first_layer(wq, picked, windows):
+            for t in range(PACK):
+                bank = psum.tile([P, S], F32, name="acc", tag="acc", bufs=4)
+                product(bank[:], wq, slice(t * P, (t + 1) * P), picked)
+                nc.scalar.copy(windows[t][:, :S], bank[:])
+
+        x_bytes = pick(xs, offs_sb, U8, "x_bytes")
+        x_codes = pick(xw, offs_sb, U32, "x_codes")
+        e_bytes = pick(es, rem_sb, U8, "e_bytes")
+        w1q = quantize(deal_weight(w1_raw, "w1_bf"), H, "w1")
+        e_codes = pick(ew, rem_sb, U32, "e_codes")
+        w2_bf = deal_weight(w2_raw, "w2_bf")
+        first_layer(w1q, (x_codes, x_bytes), y_win)
+        w2q = quantize(w2_bf, H, "w2")
+        first_layer(w2q, (e_codes, e_bytes), ye_win)
+
+        w3_bf = sb([P, N, PACK], BF16, "w3_bf")
+        nc.scalar.copy(w3_bf[:], w3_raw[:].rearrange("p j m -> p m j"))
+        w3q = quantize(w3_bf[:].rearrange("p m j -> p (m j)"), N, "w3")
+
+        gate = []
+        sums = []
+        for h in range(2):
+            part = slice(h * HALF // 16, (h + 1) * HALF // 16)
+            gq = [sb([P, HALF], F32, "gq%d" % t) for t in range(PACK)]
+            for t in range(PACK):
+                nc.vector.tensor_copy(gq[t][:], y_win[t][:].indirect(qu_sb[:, part]))
+            if h == 0:
+                for t in range(PACK):
+                    mixd = sb([P, S], F32, "mixd%d" % t)
+                    nc.vector.tensor_tensor(mixd[:], y_win[t][:].indirect(hsh_sb[:]), ye_win[t][:, :S], ALU.subtract)
+                    nc.scalar.activation(mix_win[t][:, :S], mixd[:], ACT.Copy, scale=unit_sb[:, t : t + 1])
+            squashed = sb([P, PACK, HALF], F32, "squashed%d" % h)
+            banks = []
+            for t in range(PACK):
+                emb = sb([P, HALF], F32, "emb%d_%d" % (h, t))
+                nc.vector.tensor_tensor(emb[:], ye_win[t][:].indirect(re_sb[:, part]), gq[t][:], ALU.mult)
+                emb_u = sb([P, HALF], F32, "emb_u%d_%d" % (h, t))
+                nc.scalar.activation(emb_u[:], emb[:], ACT.Copy, scale=unit_sb[:, t : t + 1])
+                nc.scalar.activation(squashed[:, t, :], emb[:], ACT.Tanh)
+                bank = psum.tile([P, HALF], F32, name="acc", tag="acc", bufs=4)
+                for b in range(HALF // BLOCK):
+                    cols = slice(b * BLOCK, (b + 1) * BLOCK)
+                    nc.tensor.matmul(bank[:, cols], emb_u[:, cols], ident[:], start=(b == 0), stop=False, is_transpose=True)
+                banks.append(bank)
+            gt = sb([P, HALF, PACK], F32, "gt%d" % h)
+            for c in range(2):
+                cols = slice(c * HALF // 2, (c + 1) * HALF // 2)
+                nc.scalar.activation(gt[:, cols, :], squashed[:, :, cols].rearrange("p t r -> p r t"), ACT.Exp, scale=0.7)
+            gate.append(gt)
+            turned = []
+            for t in range(PACK):
+                hashed = sb([P, HALF], F32, "hashed%d_%d" % (h, t))
+                nc.vector.tensor_tensor(hashed[:], mix_win[t][:].indirect(re_sb[:, part]), imp_sb[h][:, t, :], ALU.mult)
+                for b in range(HALF // BLOCK):
+                    cols = slice(b * BLOCK, (b + 1) * BLOCK)
+                    nc.tensor.matmul(
+                        banks[t][:, cols], hashed[:, cols], ident[:], start=False, stop=(b == HALF // BLOCK - 1), is_transpose=True
+                    )
+                buf = sb([P, HALF], F32, "turned%d_%d" % (h, t))
+                nc.scalar.copy(buf[:], banks[t][:])
+                turned.append(buf)
+            sums.append(turned)
+
+        first = 0
+        for g, width in enumerate(OUT_WIDTHS):
+            hid = sb([P, width, PACK], BF16, "hid%d" % g)
+            for r0 in range(first, first + width, BLOCK):
+                h, c0 = divmod(r0, HALF)
+                back = psum.tile([P, PACK, BLOCK], F32, name="back", tag="back", bufs=3)
+                for t in range(PACK):
+                    nc.tensor.transpose(back[:, t, :], sums[h][t][:, c0 : c0 + BLOCK], ident[:])
+                nc.vector.tensor_tensor(
+                    hid[:, r0 - first : r0 - first + BLOCK, :],
+                    back[:].rearrange("p t r -> p r t"),
+                    gate[h][:, c0 : c0 + BLOCK, :],
+                    ALU.mult,
+                )
+            hq = quantize(hid[:].rearrange("p r t -> p (r t)"), width, "hid%d" % g)
+            res = psum.tile([P, width], F32, name="res", tag="res", bufs=1)
+            product(res[:], w3q, slice(0, N), hq)
+            res_sb = sb([P, width], F32, "res%d" % g)
+            nc.scalar.copy(res_sb[:], res[:])
+            nc.sync.dma_start(out[:, first : first + width], res_sb[:])
+            first = first + width

@@ -33,8 +33,8 @@ def tile_picked_yqrcmp_gate_p_kernel(
         keep = ctx.enter_context(tc.tile_pool(name="keep", bufs=1))
         psum = ctx.enter_context(tc.psum_pool(name="psum", bufs=1))
 
-        def sb(shape, dtype, name):
-            return keep.tile(shape, dtype, name=name, align_bytes=64)
+        def sb(shape, dtype, name, tag=""):
+            return keep.tile(shape, dtype, name=name, tag=tag or name, align_bytes=64)
 
         def load_list(src, name):
             buf = sb(list(src.shape), U16, name)
@@ -46,9 +46,9 @@ def tile_picked_yqrcmp_gate_p_kernel(
             nc.sync.dma_start(buf[:].bitcast(I32), src[0].rearrange("p n t -> p (n t)").bitcast(I32))
             return buf
 
-        def load_scales(src, name, queue):
+        def load_scales(src, name, engine, queue):
             buf = sb([P, T], U8, name)
-            nc.vector.memset(buf[:].bitcast(I32), 0)
+            engine.memset(buf[:].bitcast(I32), 0)
             for q in range(4):
                 queue.dma_start(buf[32 * q : 32 * q + 4, :].bitcast(I32), src[0, 4 * q : 4 * q + 4, :].bitcast(I32))
             return buf
@@ -65,19 +65,19 @@ def tile_picked_yqrcmp_gate_p_kernel(
             return buf
 
         offs_sb = load_list(offs, "offs_sb")
-        xw = load_words(x_words, "xw")
-        xs = load_scales(x_scales, "xs", nc.scalar)
-        es = load_scales(e_scales, "es", nc.gpsimd)
-        w1_raw = [load_weight_half(w1, 0, "w1_raw0")]
         rem_sb = load_list(rem, "rem_sb")
-        w1_raw.append(load_weight_half(w1, 1, "w1_raw1"))
+        xs = load_scales(x_scales, "xs", nc.gpsimd, nc.sync)
+        w1_raw = [load_weight_half(w1, half, "w1_raw%d" % half) for half in range(2)]
+        y_win = [window(WIDE_WINDOW, "y%d" % t, nc.vector) for t in range(PACK)]
+        es = load_scales(e_scales, "es", nc.gpsimd, nc.sync)
+        xw = load_words(x_words, "xw")
         ew = load_words(e_words, "ew")
-        w2_raw = [load_weight_half(w2, half, "w2_raw%d" % half) for half in range(2)]
-        qu_sb = load_list(qu, "qu_sb")
-        hsh_sb = load_list(hsh, "hsh_sb")
-        re_sb = load_list(re, "re_sb")
         unit_sb = sb([P, PACK], F32, "unit_sb")
         nc.sync.dma_start(unit_sb[:], unit.rearrange("(p t) o -> p (t o)", t=PACK))
+        qu_sb = load_list(qu, "qu_sb")
+        w2_raw = [load_weight_half(w2, half, "w2_raw%d" % half) for half in range(2)]
+        hsh_sb = load_list(hsh, "hsh_sb")
+        re_sb = load_list(re, "re_sb")
         imp_sb = []
         for h in range(2):
             buf = sb([P, PACK, HALF], F32, "imp%d" % h)
@@ -86,7 +86,6 @@ def tile_picked_yqrcmp_gate_p_kernel(
         w3_raw = sb([P, PACK, N], F32, "w3_raw")
         nc.sync.dma_start(w3_raw[:], w3.rearrange("(p j) m -> p j m", j=PACK))
 
-        y_win = [window(WIDE_WINDOW, "y%d" % t, nc.vector) for t in range(PACK)]
         ye_win = [window(WINDOW, "ye%d" % t, nc.gpsimd) for t in range(PACK)]
         mix_win = [window(WINDOW, "mix%d" % t, nc.gpsimd) for t in range(PACK)]
         ident = sb([P, P], F32, "ident")
@@ -97,8 +96,8 @@ def tile_picked_yqrcmp_gate_p_kernel(
             nc.vector.tensor_copy(buf[:], table[:].indirect(offsets[:]))
             return buf
 
-        def deal_weight(raw, name):
-            buf = sb([P, PACK, P, PACK], BF16, name)
+        def deal_weight(raw, name, tag=""):
+            buf = sb([P, PACK, P, PACK], BF16, name, tag)
             for half in range(2):
                 nc.scalar.copy(
                     buf[:, :, half * (P // 2) : (half + 1) * (P // 2), :].rearrange("p t m j -> p m j t"),
@@ -106,38 +105,53 @@ def tile_picked_yqrcmp_gate_p_kernel(
                 )
             return buf[:].rearrange("p t m j -> p (t m j)")
 
-        def quantize(values, width, name):
-            codes = sb([P, width], U32, name + "_codes")
+        def quantize(values, width, name, tag=""):
+            codes = sb([P, width], U32, name + "_codes", tag)
             scales = sb([P, width], U8, name + "_scales")
             nc.vector.quantize_mx(out=codes[:].bitcast(FP8X4), scales=scales[:], in_=values)
             return codes, scales
 
-        def product(bank, lhs, cols, rhs):
+        def product(bank, lhs, cols, rhs, rhs_cols):
             nc.tensor.matmul_mx(
                 out=bank,
                 lhsT=lhs[0][:, cols].bitcast(FP8X4),
                 lhsT_scale=lhs[1][:, cols],
-                rhs=rhs[0][:].bitcast(FP8X4),
-                rhs_scale=rhs[1][:],
+                rhs=rhs[0][:, rhs_cols].bitcast(FP8X4),
+                rhs_scale=rhs[1][:, rhs_cols],
                 start=True,
                 stop=True,
             )
 
-        def first_layer(wq, picked, windows):
-            for t in range(PACK):
-                bank = psum.tile([P, S], F32, name="acc", tag="acc", bufs=4)
-                product(bank[:], wq, slice(t * P, (t + 1) * P), picked)
-                nc.scalar.copy(windows[t][:, :S], bank[:])
+        def first_layer(wq, t, picked, cols):
+            bank = psum.tile([P, cols.stop - cols.start], F32, name="acc", tag="acc", bufs=4)
+            product(bank[:], wq, slice(t * P, (t + 1) * P), picked, cols)
+            return bank
 
         x_bytes = pick(xs, offs_sb, U8, "x_bytes")
-        x_codes = pick(xw, offs_sb, U32, "x_codes")
         e_bytes = pick(es, rem_sb, U8, "e_bytes")
         w1q = quantize(deal_weight(w1_raw, "w1_bf"), H, "w1")
+        x_codes = sb([P, S], U32, "x_codes")
+        for half in range(2):
+            nc.vector.tensor_copy(
+                x_codes[:, half * S // 2 : (half + 1) * S // 2], xw[:].indirect(offs_sb[:, half * S // 32 : (half + 1) * S // 32])
+            )
         e_codes = pick(ew, rem_sb, U32, "e_codes")
-        w2_bf = deal_weight(w2_raw, "w2_bf")
-        first_layer(w1q, (x_codes, x_bytes), y_win)
-        w2q = quantize(w2_bf, H, "w2")
-        first_layer(w2q, (e_codes, e_bytes), ye_win)
+        for t in range(PACK):
+            step = S // 2 if t == 0 else S
+            for c0 in range(0, S, step):
+                cols = slice(c0, c0 + step)
+                bank = first_layer(w1q, t, (x_codes, x_bytes), cols)
+                nc.scalar.activation(y_win[t][:, cols], bank[:], ACT.Copy, scale=unit_sb[:, t : t + 1])
+        divisor = sb([P, PACK], F32, "divisor")
+        nc.vector.scalar_tensor_tensor(divisor[:], unit_sb[:], 0.0, unit_sb[:], ALU.is_equal, ALU.add)
+        undo = sb([P, PACK], F32, "undo")
+        nc.vector.reciprocal(undo[:], divisor[:])
+        w2q = quantize(deal_weight(w2_raw, "w2_bf", "w1_codes"), H, "w2")
+        ye_u = [sb([P, S], F32, "ye_u%d" % t) for t in range(PACK)]
+        for t in range(PACK):
+            bank = first_layer(w2q, t, (e_codes, e_bytes), slice(0, S))
+            nc.scalar.activation(ye_u[t][:], bank[:], ACT.Copy, scale=unit_sb[:, t : t + 1])
+            nc.scalar.copy(ye_win[t][:, :S], bank[:])
 
         w3_bf = sb([P, N, PACK], BF16, "w3_bf")
         nc.scalar.copy(w3_bf[:], w3_raw[:].rearrange("p j m -> p m j"))
@@ -147,32 +161,32 @@ def tile_picked_yqrcmp_gate_p_kernel(
         sums = []
         for h in range(2):
             part = slice(h * HALF // 16, (h + 1) * HALF // 16)
-            gq = [sb([P, HALF], F32, "gq%d" % t) for t in range(PACK)]
+            if h == 0:
+                gq = [sb([P, HALF], F32, "gq%d" % t)[:] for t in range(PACK)]
+            else:
+                early = sb([P, 2, HALF], F32, "gq_early", "w1_codes")
+                gq = [early[:, 0, :], early[:, 1, :]] + [sb([P, HALF], F32, "gq%d" % t)[:] for t in (2, 3)]
             for t in range(PACK):
-                nc.vector.tensor_copy(gq[t][:], y_win[t][:].indirect(qu_sb[:, part]))
+                nc.vector.tensor_copy(gq[t], y_win[t][:].indirect(qu_sb[:, part]))
             if h == 0:
                 for t in range(PACK):
-                    mixd = sb([P, S], F32, "mixd%d" % t)
-                    nc.vector.tensor_tensor(mixd[:], y_win[t][:].indirect(hsh_sb[:]), ye_win[t][:, :S], ALU.subtract)
-                    nc.scalar.activation(mix_win[t][:, :S], mixd[:], ACT.Copy, scale=unit_sb[:, t : t + 1])
+                    nc.vector.tensor_tensor(mix_win[t][:, :S], y_win[t][:].indirect(hsh_sb[:]), ye_u[t][:], ALU.subtract)
             squashed = sb([P, PACK, HALF], F32, "squashed%d" % h)
             banks = []
             for t in range(PACK):
                 emb = sb([P, HALF], F32, "emb%d_%d" % (h, t))
-                nc.vector.tensor_tensor(emb[:], ye_win[t][:].indirect(re_sb[:, part]), gq[t][:], ALU.mult)
-                emb_u = sb([P, HALF], F32, "emb_u%d_%d" % (h, t))
-                nc.scalar.activation(emb_u[:], emb[:], ACT.Copy, scale=unit_sb[:, t : t + 1])
-                nc.scalar.activation(squashed[:, t, :], emb[:], ACT.Tanh)
+                nc.vector.tensor_tensor(emb[:], ye_win[t][:].indirect(re_sb[:, part]), gq[t], ALU.mult)
+                nc.scalar.activation(squashed[:, t, :], emb[:], ACT.Tanh, scale=undo[:, t : t + 1])
                 bank = psum.tile([P, HALF], F32, name="acc", tag="acc", bufs=4)
                 for b in range(HALF // BLOCK):
                     cols = slice(b * BLOCK, (b + 1) * BLOCK)
-                    nc.tensor.matmul(bank[:, cols], emb_u[:, cols], ident[:], start=(b == 0), stop=False, is_transpose=True)
+                    nc.tensor.matmul(bank[:, cols], emb[:, cols], ident[:], start=(b == 0), stop=False, is_transpose=True)
                 banks.append(bank)
-            gt = sb([P, HALF, PACK], F32, "gt%d" % h)
-            for c in range(2):
-                cols = slice(c * HALF // 2, (c + 1) * HALF // 2)
-                nc.scalar.activation(gt[:, cols, :], squashed[:, :, cols].rearrange("p t r -> p r t"), ACT.Exp, scale=0.7)
-            gate.append(gt)
+            for b in range(HALF // BLOCK):
+                cols = slice(b * BLOCK, (b + 1) * BLOCK)
+                gt = sb([P, BLOCK, PACK], F32, "gt%d" % len(gate))
+                nc.scalar.activation(gt[:], squashed[:, :, cols].rearrange("p t r -> p r t"), ACT.Exp, scale=0.7)
+                gate.append(gt)
             turned = []
             for t in range(PACK):
                 hashed = sb([P, HALF], F32, "hashed%d_%d" % (h, t))
@@ -187,24 +201,35 @@ def tile_picked_yqrcmp_gate_p_kernel(
                 turned.append(buf)
             sums.append(turned)
 
-        first = 0
-        for g, width in enumerate(OUT_WIDTHS):
-            hid = sb([P, width, PACK], BF16, "hid%d" % g)
-            for r0 in range(first, first + width, BLOCK):
-                h, c0 = divmod(r0, HALF)
-                back = psum.tile([P, PACK, BLOCK], F32, name="back", tag="back", bufs=3)
-                for t in range(PACK):
-                    nc.tensor.transpose(back[:, t, :], sums[h][t][:, c0 : c0 + BLOCK], ident[:])
-                nc.vector.tensor_tensor(
-                    hid[:, r0 - first : r0 - first + BLOCK, :],
-                    back[:].rearrange("p t r -> p r t"),
-                    gate[h][:, c0 : c0 + BLOCK, :],
-                    ALU.mult,
-                )
-            hq = quantize(hid[:].rearrange("p r t -> p (r t)"), width, "hid%d" % g)
-            res = psum.tile([P, width], F32, name="res", tag="res", bufs=1)
-            product(res[:], w3q, slice(0, N), hq)
-            res_sb = sb([P, width], F32, "res%d" % g)
+        def gated_block(hid, r0, first):
+            h, c0 = divmod(r0, HALF)
+            back = psum.tile([P, PACK, BLOCK], F32, name="back", tag="back", bufs=4)
+            for t in range(PACK):
+                nc.tensor.transpose(back[:, t, :], sums[h][t][:, c0 : c0 + BLOCK], ident[:])
+            nc.vector.tensor_tensor(
+                hid[:, r0 - first : r0 - first + BLOCK, :],
+                back[:].rearrange("p t r -> p r t"),
+                gate[r0 // BLOCK][:],
+                ALU.mult,
+            )
+
+        def last_layer(hid, first, width, tag):
+            hq = quantize(hid[:].rearrange("p r t -> p (r t)"), width, "hid%d" % first, tag)
+            res = psum.tile([P, width], F32, name="res", tag="acc", bufs=4)
+            product(res[:], w3q, slice(0, N), hq, slice(0, width))
+            res_sb = sb([P, width], F32, "res%d" % first)
             nc.scalar.copy(res_sb[:], res[:])
             nc.sync.dma_start(out[:, first : first + width], res_sb[:])
+
+        first = 0
+        waiting = None
+        for width in OUT_WIDTHS:
+            hid = sb([P, width, PACK], BF16, "hid%d" % first)
+            for r0 in range(first, first + width, BLOCK):
+                gated_block(hid, r0, first)
+                if waiting is not None:
+                    last_layer(waiting[0], waiting[1], waiting[2], "gt%d" % (r0 // BLOCK))
+                    waiting = None
+            waiting = (hid, first, width)
             first = first + width
+        last_layer(waiting[0], waiting[1], waiting[2], "")

@@ -20,7 +20,6 @@ P = 128
 PACK = 4
 HALF = U // 2
 BLOCK = 128
-WIDE_WINDOW = 2 * S
 WINDOW = S + 16
 OUT_WIDTHS = (256, 256, 256, 128, 128)
 
@@ -53,11 +52,14 @@ def tile_picked_yqrcmp_gate_p_kernel(
                 queue.dma_start(buf[32 * q : 32 * q + 4, :].bitcast(I32), src[0, 4 * q : 4 * q + 4, :].bitcast(I32))
             return buf
 
-        def load_weight_half(w, half, name):
-            buf = sb([P, PACK, H // 2], F32, name)
-            cols = slice(half * (H // 2), (half + 1) * (H // 2))
-            nc.sync.dma_start(buf[:], w.rearrange("(p j) c -> p j c", j=PACK)[:, :, cols])
-            return buf
+        def load_weight(w, parts, name):
+            loaded = []
+            for part in range(parts):
+                buf = sb([P, PACK, H // parts], F32, "%s%d" % (name, part))
+                cols = slice(part * H // parts, (part + 1) * H // parts)
+                nc.sync.dma_start(buf[:], w.rearrange("(p j) c -> p j c", j=PACK)[:, :, cols])
+                loaded.append(buf)
+            return loaded
 
         def window(width, name, engine):
             buf = sb([P, width], F32, name)
@@ -67,15 +69,14 @@ def tile_picked_yqrcmp_gate_p_kernel(
         offs_sb = load_list(offs, "offs_sb")
         rem_sb = load_list(rem, "rem_sb")
         xs = load_scales(x_scales, "xs", nc.gpsimd, nc.sync)
-        w1_raw = [load_weight_half(w1, half, "w1_raw%d" % half) for half in range(2)]
-        y_win = [window(WIDE_WINDOW, "y%d" % t, nc.vector) for t in range(PACK)]
+        w1_raw = load_weight(w1, 2, "w1_raw")
         es = load_scales(e_scales, "es", nc.gpsimd, nc.sync)
         xw = load_words(x_words, "xw")
-        ew = load_words(e_words, "ew")
         unit_sb = sb([P, PACK], F32, "unit_sb")
         nc.sync.dma_start(unit_sb[:], unit.rearrange("(p t) o -> p (t o)", t=PACK))
         qu_sb = load_list(qu, "qu_sb")
-        w2_raw = [load_weight_half(w2, half, "w2_raw%d" % half) for half in range(2)]
+        ew = load_words(e_words, "ew")
+        w2_raw = load_weight(w2, 1, "w2_raw")
         hsh_sb = load_list(hsh, "hsh_sb")
         re_sb = load_list(re, "re_sb")
         imp_sb = []
@@ -86,6 +87,7 @@ def tile_picked_yqrcmp_gate_p_kernel(
         w3_raw = sb([P, PACK, N], F32, "w3_raw")
         nc.sync.dma_start(w3_raw[:], w3.rearrange("(p j) m -> p j m", j=PACK))
 
+        y_win = [window(WINDOW, "y%d" % t, nc.gpsimd) for t in range(PACK)]
         ye_win = [window(WINDOW, "ye%d" % t, nc.gpsimd) for t in range(PACK)]
         mix_win = [window(WINDOW, "mix%d" % t, nc.gpsimd) for t in range(PACK)]
         ident = sb([P, P], F32, "ident")
@@ -98,10 +100,10 @@ def tile_picked_yqrcmp_gate_p_kernel(
 
         def deal_weight(raw, name, tag=""):
             buf = sb([P, PACK, P, PACK], BF16, name, tag)
-            for half in range(2):
+            for part in range(len(raw)):
                 nc.scalar.copy(
-                    buf[:, :, half * (P // 2) : (half + 1) * (P // 2), :].rearrange("p t m j -> p m j t"),
-                    raw[half][:].rearrange("p j (m t) -> p m j t", t=PACK),
+                    buf[:, :, part * P // len(raw) : (part + 1) * P // len(raw), :].rearrange("p t m j -> p m t j"),
+                    raw[part][:].rearrange("p j (m t) -> p m t j", t=PACK),
                 )
             return buf[:].rearrange("p t m j -> p (t m j)")
 
@@ -123,7 +125,7 @@ def tile_picked_yqrcmp_gate_p_kernel(
             )
 
         def first_layer(wq, t, picked, cols):
-            bank = psum.tile([P, cols.stop - cols.start], F32, name="acc", tag="acc", bufs=4)
+            bank = psum.tile([P, cols.stop - cols.start], F32, name="acc", tag="back", bufs=4)
             product(bank[:], wq, slice(t * P, (t + 1) * P), picked, cols)
             return bank
 
@@ -142,51 +144,55 @@ def tile_picked_yqrcmp_gate_p_kernel(
                 cols = slice(c0, c0 + step)
                 bank = first_layer(w1q, t, (x_codes, x_bytes), cols)
                 nc.scalar.activation(y_win[t][:, cols], bank[:], ACT.Copy, scale=unit_sb[:, t : t + 1])
+        is_zero = sb([P, PACK], F32, "is_zero")
+        nc.gpsimd.tensor_scalar(is_zero[:], unit_sb[:], 0.0, None, ALU.is_equal)
         divisor = sb([P, PACK], F32, "divisor")
-        nc.vector.scalar_tensor_tensor(divisor[:], unit_sb[:], 0.0, unit_sb[:], ALU.is_equal, ALU.add)
+        nc.gpsimd.tensor_tensor(divisor[:], is_zero[:], unit_sb[:], ALU.add)
         undo = sb([P, PACK], F32, "undo")
         nc.vector.reciprocal(undo[:], divisor[:])
+        minus_unit = sb([P, PACK], F32, "minus_unit")
+        nc.scalar.activation(minus_unit[:], unit_sb[:], ACT.Copy, scale=-1.0)
         w2q = quantize(deal_weight(w2_raw, "w2_bf", "w1_codes"), H, "w2")
         ye_u = [sb([P, S], F32, "ye_u%d" % t) for t in range(PACK)]
         for t in range(PACK):
             bank = first_layer(w2q, t, (e_codes, e_bytes), slice(0, S))
-            nc.scalar.activation(ye_u[t][:], bank[:], ACT.Copy, scale=unit_sb[:, t : t + 1])
+            nc.scalar.activation(ye_u[t][:], bank[:], ACT.Copy, scale=minus_unit[:, t : t + 1])
             nc.scalar.copy(ye_win[t][:, :S], bank[:])
 
-        w3_bf = sb([P, N, PACK], BF16, "w3_bf")
+        w3_bf = sb([P, N, PACK], BF16, "w3_bf", "w2_codes")
         nc.scalar.copy(w3_bf[:], w3_raw[:].rearrange("p j m -> p m j"))
         w3q = quantize(w3_bf[:].rearrange("p m j -> p (m j)"), N, "w3")
 
         gate = []
+        idents = [ident]
         sums = []
         for h in range(2):
             part = slice(h * HALF // 16, (h + 1) * HALF // 16)
             if h == 0:
                 gq = [sb([P, HALF], F32, "gq%d" % t)[:] for t in range(PACK)]
             else:
-                early = sb([P, 2, HALF], F32, "gq_early", "w1_codes")
-                gq = [early[:, 0, :], early[:, 1, :]] + [sb([P, HALF], F32, "gq%d" % t)[:] for t in (2, 3)]
+                held = sb([P, PACK - 1, HALF], F32, "gq_held", "w1_codes")
+                gq = [sb([P, HALF], F32, "gq_free")[:]] + [held[:, t, :] for t in range(PACK - 1)]
             for t in range(PACK):
                 nc.vector.tensor_copy(gq[t], y_win[t][:].indirect(qu_sb[:, part]))
             if h == 0:
                 for t in range(PACK):
-                    nc.vector.tensor_tensor(mix_win[t][:, :S], y_win[t][:].indirect(hsh_sb[:]), ye_u[t][:], ALU.subtract)
+                    nc.vector.tensor_tensor(mix_win[t][:, :S], y_win[t][:].indirect(hsh_sb[:]), ye_u[t][:], ALU.add)
             squashed = sb([P, PACK, HALF], F32, "squashed%d" % h)
-            banks = []
+            banks = [psum.tile([P, HALF], F32, name="acc", tag="acc", bufs=4) for t in range(PACK)]
             for t in range(PACK):
                 emb = sb([P, HALF], F32, "emb%d_%d" % (h, t))
                 nc.vector.tensor_tensor(emb[:], ye_win[t][:].indirect(re_sb[:, part]), gq[t], ALU.mult)
                 nc.scalar.activation(squashed[:, t, :], emb[:], ACT.Tanh, scale=undo[:, t : t + 1])
-                bank = psum.tile([P, HALF], F32, name="acc", tag="acc", bufs=4)
                 for b in range(HALF // BLOCK):
                     cols = slice(b * BLOCK, (b + 1) * BLOCK)
-                    nc.tensor.matmul(bank[:, cols], emb[:, cols], ident[:], start=(b == 0), stop=False, is_transpose=True)
-                banks.append(bank)
+                    nc.tensor.matmul(banks[t][:, cols], emb[:, cols], idents[h][:], start=(b == 0), stop=False, is_transpose=True)
             for b in range(HALF // BLOCK):
                 cols = slice(b * BLOCK, (b + 1) * BLOCK)
                 gt = sb([P, BLOCK, PACK], F32, "gt%d" % len(gate))
                 nc.scalar.activation(gt[:], squashed[:, :, cols].rearrange("p t r -> p r t"), ACT.Exp, scale=0.7)
                 gate.append(gt)
+            backs = [psum.tile([P, HALF], F32, name="back", tag=("back", "acc")[h], bufs=4)[:] for b in range(PACK)]
             turned = []
             for t in range(PACK):
                 hashed = sb([P, HALF], F32, "hashed%d_%d" % (h, t))
@@ -194,42 +200,47 @@ def tile_picked_yqrcmp_gate_p_kernel(
                 for b in range(HALF // BLOCK):
                     cols = slice(b * BLOCK, (b + 1) * BLOCK)
                     nc.tensor.matmul(
-                        banks[t][:, cols], hashed[:, cols], ident[:], start=False, stop=(b == HALF // BLOCK - 1), is_transpose=True
+                        banks[t][:, cols], hashed[:, cols], idents[h][:], start=False, stop=(b == HALF // BLOCK - 1), is_transpose=True
                     )
                 buf = sb([P, HALF], F32, "turned%d_%d" % (h, t))
                 nc.scalar.copy(buf[:], banks[t][:])
                 turned.append(buf)
-            sums.append(turned)
+                for b in range(PACK):
+                    for u in range(PACK):
+                        if (max(b, u) if h == 1 else u) == t:
+                            nc.tensor.transpose(
+                                backs[b][:, u * BLOCK : (u + 1) * BLOCK], turned[u][:, b * BLOCK : (b + 1) * BLOCK], ident[:]
+                            )
+            sums.extend(backs)
+            if h == 0:
+                late = sb([P, P], F32, "late_ident", "hashed0_%d" % (PACK - 1))
+                nc.scalar.copy(late[:], ident[:])
+                idents.append(late)
 
         def gated_block(hid, r0, first):
-            h, c0 = divmod(r0, HALF)
-            back = psum.tile([P, PACK, BLOCK], F32, name="back", tag="back", bufs=4)
-            for t in range(PACK):
-                nc.tensor.transpose(back[:, t, :], sums[h][t][:, c0 : c0 + BLOCK], ident[:])
             nc.vector.tensor_tensor(
                 hid[:, r0 - first : r0 - first + BLOCK, :],
-                back[:].rearrange("p t r -> p r t"),
+                sums[r0 // BLOCK].rearrange("p (t r) -> p r t", t=PACK),
                 gate[r0 // BLOCK][:],
                 ALU.mult,
             )
 
-        def last_layer(hid, first, width, tag):
-            hq = quantize(hid[:].rearrange("p r t -> p (r t)"), width, "hid%d" % first, tag)
-            res = psum.tile([P, width], F32, name="res", tag="acc", bufs=4)
+        def last_layer(hid, first, width, copy):
+            hq = quantize(hid[:].rearrange("p r t -> p (r t)"), width, "hid%d" % first)
+            res = psum.tile([P, width], F32, name="res", tag="acc" if first < HALF else "back", bufs=4)
             product(res[:], w3q, slice(0, N), hq, slice(0, width))
             res_sb = sb([P, width], F32, "res%d" % first)
-            nc.scalar.copy(res_sb[:], res[:])
+            copy(res_sb[:], res[:])
             nc.sync.dma_start(out[:, first : first + width], res_sb[:])
 
+        groups = []
         first = 0
-        waiting = None
         for width in OUT_WIDTHS:
-            hid = sb([P, width, PACK], BF16, "hid%d" % first)
+            hid = sb([P, width, PACK], BF16, "hid%d" % first, {0: "mix2", 256: "mix1"}.get(first, ""))
             for r0 in range(first, first + width, BLOCK):
                 gated_block(hid, r0, first)
-                if waiting is not None:
-                    last_layer(waiting[0], waiting[1], waiting[2], "gt%d" % (r0 // BLOCK))
-                    waiting = None
-            waiting = (hid, first, width)
+            groups.append((hid, first, width))
             first = first + width
-        last_layer(waiting[0], waiting[1], waiting[2], "")
+        for hid, first, width in groups:
+            copy = nc.vector.tensor_copy if width == BLOCK else nc.scalar.copy
+            last_layer(hid, first, width, copy)

@@ -4,7 +4,7 @@ import concourse.mybir as mybir
 from concourse.masks import make_identity
 
 K, T, S, N, H, U = 512, 1024, 512, 128, 512, 1024
-FLOPS = 2 * K * H * S * 2 + 2 * H * N * U
+FLOPS = 2 * (2 * K * H * S) + 2 * H * N * U
 
 F32 = mybir.dt.float32
 BF16 = mybir.dt.bfloat16
@@ -18,9 +18,13 @@ ALU = mybir.AluOpType
 
 P = 128
 PACK = 4
+LIST_ROWS = 16
 HALF = U // 2
 BLOCK = 128
+BLOCKS = HALF // BLOCK
 WINDOW = S + 16
+BANKS = 4
+W1_PARTS = 2
 OUT_WIDTHS = (256, 256, 256, 128, 128)
 
 
@@ -32,8 +36,8 @@ def tile_picked_yqrcmp_gate_p_kernel(
         keep = ctx.enter_context(tc.tile_pool(name="keep", bufs=1))
         psum = ctx.enter_context(tc.psum_pool(name="psum", bufs=1))
 
-        def sb(shape, dtype, name, tag=""):
-            return keep.tile(shape, dtype, name=name, tag=tag or name, align_bytes=64)
+        def sb(shape, dtype, name, reuse=""):
+            return keep.tile(shape, dtype, name=name, tag=reuse or name, align_bytes=64)
 
         def load_list(src, name):
             buf = sb(list(src.shape), U16, name)
@@ -45,11 +49,11 @@ def tile_picked_yqrcmp_gate_p_kernel(
             nc.sync.dma_start(buf[:].bitcast(I32), src[0].rearrange("p n t -> p (n t)").bitcast(I32))
             return buf
 
-        def load_scales(src, name, engine, queue):
+        def load_scales(src, name):
             buf = sb([P, T], U8, name)
-            engine.memset(buf[:].bitcast(I32), 0)
+            nc.gpsimd.memset(buf[:].bitcast(I32), 0)
             for q in range(4):
-                queue.dma_start(buf[32 * q : 32 * q + 4, :].bitcast(I32), src[0, 4 * q : 4 * q + 4, :].bitcast(I32))
+                nc.sync.dma_start(buf[32 * q : 32 * q + 4, :].bitcast(I32), src[0, 4 * q : 4 * q + 4, :].bitcast(I32))
             return buf
 
         def load_weight(w, parts, name):
@@ -61,21 +65,21 @@ def tile_picked_yqrcmp_gate_p_kernel(
                 loaded.append(buf)
             return loaded
 
-        def window(width, name, engine):
-            buf = sb([P, width], F32, name)
-            engine.memset(buf[:, S:], 0.0)
+        def window(name):
+            buf = sb([P, WINDOW], F32, name)
+            nc.gpsimd.memset(buf[:, S:], 0.0)
             return buf
 
         offs_sb = load_list(offs, "offs_sb")
         rem_sb = load_list(rem, "rem_sb")
-        xs = load_scales(x_scales, "xs", nc.gpsimd, nc.sync)
-        w1_raw = load_weight(w1, 2, "w1_raw")
-        es = load_scales(e_scales, "es", nc.gpsimd, nc.sync)
-        xw = load_words(x_words, "xw")
+        x_scale_table = load_scales(x_scales, "x_scale_table")
+        w1_raw = load_weight(w1, W1_PARTS, "w1_raw")
+        e_scale_table = load_scales(e_scales, "e_scale_table")
+        x_word_table = load_words(x_words, "x_word_table")
+        e_word_table = load_words(e_words, "e_word_table")
         unit_sb = sb([P, PACK], F32, "unit_sb")
         nc.sync.dma_start(unit_sb[:], unit.rearrange("(p t) o -> p (t o)", t=PACK))
         qu_sb = load_list(qu, "qu_sb")
-        ew = load_words(e_words, "ew")
         w2_raw = load_weight(w2, 1, "w2_raw")
         hsh_sb = load_list(hsh, "hsh_sb")
         re_sb = load_list(re, "re_sb")
@@ -87,9 +91,9 @@ def tile_picked_yqrcmp_gate_p_kernel(
         w3_raw = sb([P, PACK, N], F32, "w3_raw")
         nc.sync.dma_start(w3_raw[:], w3.rearrange("(p j) m -> p j m", j=PACK))
 
-        y_win = [window(WINDOW, "y%d" % t, nc.gpsimd) for t in range(PACK)]
-        ye_win = [window(WINDOW, "ye%d" % t, nc.gpsimd) for t in range(PACK)]
-        mix_win = [window(WINDOW, "mix%d" % t, nc.gpsimd) for t in range(PACK)]
+        yu_win = [window("yu%d" % t) for t in range(PACK)]
+        ye_win = [window("ye%d" % t) for t in range(PACK)]
+        mix_win = [window("mix%d" % t) for t in range(PACK)]
         ident = sb([P, P], F32, "ident")
         make_identity(nc, ident[:])
 
@@ -98,8 +102,8 @@ def tile_picked_yqrcmp_gate_p_kernel(
             nc.vector.tensor_copy(buf[:], table[:].indirect(offsets[:]))
             return buf
 
-        def deal_weight(raw, name, tag=""):
-            buf = sb([P, PACK, P, PACK], BF16, name, tag)
+        def deal_weight(raw, name, reuse=""):
+            buf = sb([P, PACK, P, PACK], BF16, name, reuse)
             for part in range(len(raw)):
                 nc.scalar.copy(
                     buf[:, :, part * P // len(raw) : (part + 1) * P // len(raw), :].rearrange("p t m j -> p m t j"),
@@ -107,17 +111,17 @@ def tile_picked_yqrcmp_gate_p_kernel(
                 )
             return buf[:].rearrange("p t m j -> p (t m j)")
 
-        def quantize(values, width, name, tag=""):
-            codes = sb([P, width], U32, name + "_codes", tag)
+        def quantize(values, width, name):
+            codes = sb([P, width], U32, name + "_codes")
             scales = sb([P, width], U8, name + "_scales")
             nc.vector.quantize_mx(out=codes[:].bitcast(FP8X4), scales=scales[:], in_=values)
             return codes, scales
 
-        def product(bank, lhs, cols, rhs, rhs_cols):
+        def product(bank, lhs, lhs_cols, rhs, rhs_cols):
             nc.tensor.matmul_mx(
                 out=bank,
-                lhsT=lhs[0][:, cols].bitcast(FP8X4),
-                lhsT_scale=lhs[1][:, cols],
+                lhsT=lhs[0][:, lhs_cols].bitcast(FP8X4),
+                lhsT_scale=lhs[1][:, lhs_cols],
                 rhs=rhs[0][:, rhs_cols].bitcast(FP8X4),
                 rhs_scale=rhs[1][:, rhs_cols],
                 start=True,
@@ -125,87 +129,90 @@ def tile_picked_yqrcmp_gate_p_kernel(
             )
 
         def first_layer(wq, t, picked, cols):
-            bank = psum.tile([P, cols.stop - cols.start], F32, name="acc", tag="back", bufs=4)
+            bank = psum.tile([P, cols.stop - cols.start], F32, name="plane", tag="back", bufs=BANKS)
             product(bank[:], wq, slice(t * P, (t + 1) * P), picked, cols)
             return bank
 
-        x_bytes = pick(xs, offs_sb, U8, "x_bytes")
-        e_bytes = pick(es, rem_sb, U8, "e_bytes")
+        x_bytes = pick(x_scale_table, offs_sb, U8, "x_bytes")
+        e_bytes = pick(e_scale_table, rem_sb, U8, "e_bytes")
         w1q = quantize(deal_weight(w1_raw, "w1_bf"), H, "w1")
         x_codes = sb([P, S], U32, "x_codes")
-        for half in range(2):
-            nc.vector.tensor_copy(
-                x_codes[:, half * S // 2 : (half + 1) * S // 2], xw[:].indirect(offs_sb[:, half * S // 32 : (half + 1) * S // 32])
-            )
-        e_codes = pick(ew, rem_sb, U32, "e_codes")
+        for c0 in range(0, S, S // 2):
+            offsets = offs_sb[:, c0 // LIST_ROWS : (c0 + S // 2) // LIST_ROWS]
+            nc.vector.tensor_copy(x_codes[:, c0 : c0 + S // 2], x_word_table[:].indirect(offsets))
+        e_codes = pick(e_word_table, rem_sb, U32, "e_codes")
         for t in range(PACK):
             step = S // 2 if t == 0 else S
             for c0 in range(0, S, step):
                 cols = slice(c0, c0 + step)
                 bank = first_layer(w1q, t, (x_codes, x_bytes), cols)
-                nc.scalar.activation(y_win[t][:, cols], bank[:], ACT.Copy, scale=unit_sb[:, t : t + 1])
+                nc.scalar.activation(yu_win[t][:, cols], bank[:], ACT.Copy, scale=unit_sb[:, t : t + 1])
+
         is_zero = sb([P, PACK], F32, "is_zero")
         nc.gpsimd.tensor_scalar(is_zero[:], unit_sb[:], 0.0, None, ALU.is_equal)
         divisor = sb([P, PACK], F32, "divisor")
         nc.gpsimd.tensor_tensor(divisor[:], is_zero[:], unit_sb[:], ALU.add)
-        undo = sb([P, PACK], F32, "undo")
-        nc.vector.reciprocal(undo[:], divisor[:])
+        inv_unit = sb([P, PACK], F32, "inv_unit")
+        nc.vector.reciprocal(inv_unit[:], divisor[:])
         minus_unit = sb([P, PACK], F32, "minus_unit")
         nc.scalar.activation(minus_unit[:], unit_sb[:], ACT.Copy, scale=-1.0)
+
         w2q = quantize(deal_weight(w2_raw, "w2_bf", "w1_codes"), H, "w2")
-        ye_u = [sb([P, S], F32, "ye_u%d" % t) for t in range(PACK)]
+        minus_yeu = [sb([P, S], F32, "minus_yeu%d" % t) for t in range(PACK)]
         for t in range(PACK):
             bank = first_layer(w2q, t, (e_codes, e_bytes), slice(0, S))
-            nc.scalar.activation(ye_u[t][:], bank[:], ACT.Copy, scale=minus_unit[:, t : t + 1])
+            nc.scalar.activation(minus_yeu[t][:], bank[:], ACT.Copy, scale=minus_unit[:, t : t + 1])
             nc.scalar.copy(ye_win[t][:, :S], bank[:])
 
         w3_bf = sb([P, N, PACK], BF16, "w3_bf", "w2_codes")
         nc.scalar.copy(w3_bf[:], w3_raw[:].rearrange("p j m -> p m j"))
         w3q = quantize(w3_bf[:].rearrange("p m j -> p (m j)"), N, "w3")
 
-        gate = []
-        idents = [ident]
+        gates = []
         sums = []
+        idents = [ident]
         for h in range(2):
-            part = slice(h * HALF // 16, (h + 1) * HALF // 16)
+            part = slice(h * HALF // LIST_ROWS, (h + 1) * HALF // LIST_ROWS)
             if h == 0:
                 gq = [sb([P, HALF], F32, "gq%d" % t)[:] for t in range(PACK)]
             else:
                 held = sb([P, PACK - 1, HALF], F32, "gq_held", "w1_codes")
                 gq = [sb([P, HALF], F32, "gq_free")[:]] + [held[:, t, :] for t in range(PACK - 1)]
             for t in range(PACK):
-                nc.vector.tensor_copy(gq[t], y_win[t][:].indirect(qu_sb[:, part]))
+                nc.vector.tensor_copy(gq[t], yu_win[t][:].indirect(qu_sb[:, part]))
             if h == 0:
                 for t in range(PACK):
-                    nc.vector.tensor_tensor(mix_win[t][:, :S], y_win[t][:].indirect(hsh_sb[:]), ye_u[t][:], ALU.add)
+                    nc.vector.tensor_tensor(mix_win[t][:, :S], yu_win[t][:].indirect(hsh_sb[:]), minus_yeu[t][:], ALU.add)
+
             squashed = sb([P, PACK, HALF], F32, "squashed%d" % h)
-            banks = [psum.tile([P, HALF], F32, name="acc", tag="acc", bufs=4) for t in range(PACK)]
+            banks = [psum.tile([P, HALF], F32, name="acc", tag="acc", bufs=BANKS) for t in range(PACK)]
             for t in range(PACK):
                 emb = sb([P, HALF], F32, "emb%d_%d" % (h, t))
                 nc.vector.tensor_tensor(emb[:], ye_win[t][:].indirect(re_sb[:, part]), gq[t], ALU.mult)
-                nc.scalar.activation(squashed[:, t, :], emb[:], ACT.Tanh, scale=undo[:, t : t + 1])
-                for b in range(HALF // BLOCK):
+                nc.scalar.activation(squashed[:, t, :], emb[:], ACT.Tanh, scale=inv_unit[:, t : t + 1])
+                for b in range(BLOCKS):
                     cols = slice(b * BLOCK, (b + 1) * BLOCK)
                     nc.tensor.matmul(banks[t][:, cols], emb[:, cols], idents[h][:], start=(b == 0), stop=False, is_transpose=True)
-            for b in range(HALF // BLOCK):
+            for b in range(BLOCKS):
                 cols = slice(b * BLOCK, (b + 1) * BLOCK)
-                gt = sb([P, BLOCK, PACK], F32, "gt%d" % len(gate))
-                nc.scalar.activation(gt[:], squashed[:, :, cols].rearrange("p t r -> p r t"), ACT.Exp, scale=0.7)
-                gate.append(gt)
-            backs = [psum.tile([P, HALF], F32, name="back", tag=("back", "acc")[h], bufs=4)[:] for b in range(PACK)]
+                gate = sb([P, BLOCK, PACK], F32, "gate%d" % len(gates))
+                nc.scalar.activation(gate[:], squashed[:, :, cols].rearrange("p t r -> p r t"), ACT.Exp, scale=0.7)
+                gates.append(gate)
+
+            backs = [psum.tile([P, HALF], F32, name="back", tag=("back", "acc")[h], bufs=BANKS)[:] for b in range(BLOCKS)]
             turned = []
             for t in range(PACK):
                 hashed = sb([P, HALF], F32, "hashed%d_%d" % (h, t))
                 nc.vector.tensor_tensor(hashed[:], mix_win[t][:].indirect(re_sb[:, part]), imp_sb[h][:, t, :], ALU.mult)
-                for b in range(HALF // BLOCK):
+                for b in range(BLOCKS):
                     cols = slice(b * BLOCK, (b + 1) * BLOCK)
                     nc.tensor.matmul(
-                        banks[t][:, cols], hashed[:, cols], idents[h][:], start=False, stop=(b == HALF // BLOCK - 1), is_transpose=True
+                        banks[t][:, cols], hashed[:, cols], idents[h][:], start=False, stop=(b == BLOCKS - 1), is_transpose=True
                     )
                 buf = sb([P, HALF], F32, "turned%d_%d" % (h, t))
                 nc.scalar.copy(buf[:], banks[t][:])
                 turned.append(buf)
-                for b in range(PACK):
+                for b in range(BLOCKS):
                     for u in range(PACK):
                         if (max(b, u) if h == 1 else u) == t:
                             nc.tensor.transpose(
@@ -213,34 +220,30 @@ def tile_picked_yqrcmp_gate_p_kernel(
                             )
             sums.extend(backs)
             if h == 0:
-                late = sb([P, P], F32, "late_ident", "hashed0_%d" % (PACK - 1))
-                nc.scalar.copy(late[:], ident[:])
-                idents.append(late)
+                late_ident = sb([P, P], F32, "late_ident", "hashed0_%d" % (PACK - 1))
+                nc.scalar.copy(late_ident[:], ident[:])
+                idents.append(late_ident)
 
-        def gated_block(hid, r0, first):
-            nc.vector.tensor_tensor(
-                hid[:, r0 - first : r0 - first + BLOCK, :],
-                sums[r0 // BLOCK].rearrange("p (t r) -> p r t", t=PACK),
-                gate[r0 // BLOCK][:],
-                ALU.mult,
-            )
-
-        def last_layer(hid, first, width, copy):
-            hq = quantize(hid[:].rearrange("p r t -> p (r t)"), width, "hid%d" % first)
-            res = psum.tile([P, width], F32, name="res", tag="acc" if first < HALF else "back", bufs=4)
-            product(res[:], w3q, slice(0, N), hq, slice(0, width))
-            res_sb = sb([P, width], F32, "res%d" % first)
-            copy(res_sb[:], res[:])
-            nc.sync.dma_start(out[:, first : first + width], res_sb[:])
-
+        after_gathers = {0: "mix2", OUT_WIDTHS[0]: "mix1"}
         groups = []
         first = 0
         for width in OUT_WIDTHS:
-            hid = sb([P, width, PACK], BF16, "hid%d" % first, {0: "mix2", 256: "mix1"}.get(first, ""))
+            hid = sb([P, width, PACK], BF16, "hid%d" % first, after_gathers.get(first, ""))
             for r0 in range(first, first + width, BLOCK):
-                gated_block(hid, r0, first)
+                nc.vector.tensor_tensor(
+                    hid[:, r0 - first : r0 - first + BLOCK, :],
+                    sums[r0 // BLOCK].rearrange("p (t r) -> p r t", t=PACK),
+                    gates[r0 // BLOCK][:],
+                    ALU.mult,
+                )
             groups.append((hid, first, width))
             first = first + width
+
         for hid, first, width in groups:
-            copy = nc.vector.tensor_copy if width == BLOCK else nc.scalar.copy
-            last_layer(hid, first, width, copy)
+            hq = quantize(hid[:].rearrange("p r t -> p (r t)"), width, "hid%d" % first)
+            res = psum.tile([P, width], F32, name="res", tag="acc" if first < HALF else "back", bufs=BANKS)
+            product(res[:], w3q, slice(0, N), hq, slice(0, width))
+            res_sb = sb([P, width], F32, "res%d" % first)
+            copy_out = nc.vector.tensor_copy if width == BLOCK else nc.scalar.copy
+            copy_out(res_sb[:], res[:])
+            nc.sync.dma_start(out[:, first : first + width], res_sb[:])

from contextlib import ExitStack

import concourse.mybir as mybir
from concourse.masks import make_identity

K, T, S, N, H, U = 512, 1024, 512, 128, 512, 1024
FLOPS = 2 * (2 * K * H * S) + 2 * H * N * U

F32 = mybir.dt.float32
BF16 = mybir.dt.bfloat16
I32 = mybir.dt.int32
U32 = mybir.dt.uint32
U16 = mybir.dt.uint16
U8 = mybir.dt.uint8
FP8X4 = mybir.dt.float8_e4m3fn_x4
ACT = mybir.ActivationFunctionType
ALU = mybir.AluOpType

P = 128
PACK = 4
LIST_ROWS = 16
HALF = U // 2
BLOCK = 128
BLOCKS = HALF // BLOCK
WINDOW = S + 16
BANKS = 4
W1_PARTS = 2
OUT_WIDTHS = (256, 256, 256, 128, 128)


def tile_picked_yqrcmp_gate_p_kernel(
    tc, x_words, x_scales, w1, e_words, e_scales, w2, imp, unit, w3, offs, rem, qu, re, hsh, out
):
    nc = tc.nc
    with ExitStack() as ctx:
        keep = ctx.enter_context(tc.tile_pool(name="keep", bufs=1))
        psum = ctx.enter_context(tc.psum_pool(name="psum", bufs=1))

        def sb(shape, dtype, name, reuse=""):
            return keep.tile(shape, dtype, name=name, tag=reuse or name, align_bytes=64)

        def load_list(src, name):
            buf = sb(list(src.shape), U16, name)
            nc.sync.dma_start(buf[:], src)
            return buf

        def load_words(src, name):
            buf = sb([P, T], U32, name)
            nc.sync.dma_start(buf[:].bitcast(I32), src[0].rearrange("p n t -> p (n t)").bitcast(I32))
            return buf

        def load_scales(src, name):
            buf = sb([P, T], U8, name)
            nc.gpsimd.memset(buf[:].bitcast(I32), 0)
            for q in range(4):
                nc.sync.dma_start(buf[32 * q : 32 * q + 4, :].bitcast(I32), src[0, 4 * q : 4 * q + 4, :].bitcast(I32))
            return buf

        def load_weight(w, parts, name):
            loaded = []
            for part in range(parts):
                buf = sb([P, PACK, H // parts], F32, "%s%d" % (name, part))
                cols = slice(part * H // parts, (part + 1) * H // parts)
                nc.sync.dma_start(buf[:], w.rearrange("(p j) c -> p j c", j=PACK)[:, :, cols])
                loaded.append(buf)
            return loaded

        def window(name):
            buf = sb([P, WINDOW], F32, name)
            nc.gpsimd.memset(buf[:, S:], 0.0)
            return buf

        offs_sb = load_list(offs, "offs_sb")
        rem_sb = load_list(rem, "rem_sb")
        x_scale_table = load_scales(x_scales, "x_scale_table")
        w1_raw = load_weight(w1, W1_PARTS, "w1_raw")
        e_scale_table = load_scales(e_scales, "e_scale_table")
        x_word_table = load_words(x_words, "x_word_table")
        e_word_table = load_words(e_words, "e_word_table")
        unit_sb = sb([P, PACK], F32, "unit_sb")
        nc.sync.dma_start(unit_sb[:], unit.rearrange("(p t) o -> p (t o)", t=PACK))
        qu_sb = load_list(qu, "qu_sb")
        w2_raw = load_weight(w2, 1, "w2_raw")
        hsh_sb = load_list(hsh, "hsh_sb")
        re_sb = load_list(re, "re_sb")
        imp_sb = []
        for h in range(2):
            buf = sb([P, PACK, HALF], F32, "imp%d" % h)
            nc.sync.dma_start(buf[:], imp.rearrange("(p t) r -> p t r", t=PACK)[:, :, h * HALF : (h + 1) * HALF])
            imp_sb.append(buf)
        w3_raw = sb([P, PACK, N], F32, "w3_raw")
        nc.sync.dma_start(w3_raw[:], w3.rearrange("(p j) m -> p j m", j=PACK))

        yu_win = [window("yu%d" % t) for t in range(PACK)]
        ye_win = [window("ye%d" % t) for t in range(PACK)]
        mix_win = [window("mix%d" % t) for t in range(PACK)]
        ident = sb([P, P], F32, "ident")
        make_identity(nc, ident[:])

        def pick(table, offsets, dtype, name):
            buf = sb([P, S], dtype, name)
            nc.vector.tensor_copy(buf[:], table[:].indirect(offsets[:]))
            return buf

        def deal_weight(raw, name, reuse=""):
            buf = sb([P, PACK, P, PACK], BF16, name, reuse)
            for part in range(len(raw)):
                nc.scalar.copy(
                    buf[:, :, part * P // len(raw) : (part + 1) * P // len(raw), :].rearrange("p t m j -> p m t j"),
                    raw[part][:].rearrange("p j (m t) -> p m t j", t=PACK),
                )
            return buf[:].rearrange("p t m j -> p (t m j)")

        def quantize(values, width, name):
            codes = sb([P, width], U32, name + "_codes")
            scales = sb([P, width], U8, name + "_scales")
            nc.vector.quantize_mx(out=codes[:].bitcast(FP8X4), scales=scales[:], in_=values)
            return codes, scales

        def product(bank, lhs, lhs_cols, rhs, rhs_cols):
            nc.tensor.matmul_mx(
                out=bank,
                lhsT=lhs[0][:, lhs_cols].bitcast(FP8X4),
                lhsT_scale=lhs[1][:, lhs_cols],
                rhs=rhs[0][:, rhs_cols].bitcast(FP8X4),
                rhs_scale=rhs[1][:, rhs_cols],
                start=True,
                stop=True,
            )

        def first_layer(wq, t, picked, cols):
            bank = psum.tile([P, cols.stop - cols.start], F32, name="plane", tag="back", bufs=BANKS)
            product(bank[:], wq, slice(t * P, (t + 1) * P), picked, cols)
            return bank

        x_bytes = pick(x_scale_table, offs_sb, U8, "x_bytes")
        e_bytes = pick(e_scale_table, rem_sb, U8, "e_bytes")
        w1q = quantize(deal_weight(w1_raw, "w1_bf"), H, "w1")
        x_codes = sb([P, S], U32, "x_codes")
        for c0 in range(0, S, S // 2):
            offsets = offs_sb[:, c0 // LIST_ROWS : (c0 + S // 2) // LIST_ROWS]
            nc.vector.tensor_copy(x_codes[:, c0 : c0 + S // 2], x_word_table[:].indirect(offsets))
        e_codes = pick(e_word_table, rem_sb, U32, "e_codes")
        for t in range(PACK):
            step = S // 2 if t == 0 else S
            for c0 in range(0, S, step):
                cols = slice(c0, c0 + step)
                bank = first_layer(w1q, t, (x_codes, x_bytes), cols)
                nc.scalar.activation(yu_win[t][:, cols], bank[:], ACT.Copy, scale=unit_sb[:, t : t + 1])

        is_zero = sb([P, PACK], F32, "is_zero")
        nc.gpsimd.tensor_scalar(is_zero[:], unit_sb[:], 0.0, None, ALU.is_equal)
        divisor = sb([P, PACK], F32, "divisor")
        nc.gpsimd.tensor_tensor(divisor[:], is_zero[:], unit_sb[:], ALU.add)
        inv_unit = sb([P, PACK], F32, "inv_unit")
        nc.vector.reciprocal(inv_unit[:], divisor[:])
        minus_unit = sb([P, PACK], F32, "minus_unit")
        nc.scalar.activation(minus_unit[:], unit_sb[:], ACT.Copy, scale=-1.0)

        w2q = quantize(deal_weight(w2_raw, "w2_bf", "w1_codes"), H, "w2")
        minus_yeu = [sb([P, S], F32, "minus_yeu%d" % t) for t in range(PACK)]
        for t in range(PACK):
            bank = first_layer(w2q, t, (e_codes, e_bytes), slice(0, S))
            nc.scalar.activation(minus_yeu[t][:], bank[:], ACT.Copy, scale=minus_unit[:, t : t + 1])
            nc.scalar.copy(ye_win[t][:, :S], bank[:])

        w3_bf = sb([P, N, PACK], BF16, "w3_bf", "w2_codes")
        nc.scalar.copy(w3_bf[:], w3_raw[:].rearrange("p j m -> p m j"))
        w3q = quantize(w3_bf[:].rearrange("p m j -> p (m j)"), N, "w3")

        gates = []
        sums = []
        idents = [ident]
        for h in range(2):
            part = slice(h * HALF // LIST_ROWS, (h + 1) * HALF // LIST_ROWS)
            if h == 0:
                gq = [sb([P, HALF], F32, "gq%d" % t)[:] for t in range(PACK)]
            else:
                held = sb([P, PACK - 1, HALF], F32, "gq_held", "w1_codes")
                gq = [sb([P, HALF], F32, "gq_free")[:]] + [held[:, t, :] for t in range(PACK - 1)]
            for t in range(PACK):
                nc.vector.tensor_copy(gq[t], yu_win[t][:].indirect(qu_sb[:, part]))
            if h == 0:
                for t in range(PACK):
                    nc.vector.tensor_tensor(mix_win[t][:, :S], yu_win[t][:].indirect(hsh_sb[:]), minus_yeu[t][:], ALU.add)

            squashed = sb([P, PACK, HALF], F32, "squashed%d" % h)
            banks = [psum.tile([P, HALF], F32, name="acc", tag="acc", bufs=BANKS) for t in range(PACK)]
            for t in range(PACK):
                emb = sb([P, HALF], F32, "emb%d_%d" % (h, t))
                nc.vector.tensor_tensor(emb[:], ye_win[t][:].indirect(re_sb[:, part]), gq[t], ALU.mult)
                nc.scalar.activation(squashed[:, t, :], emb[:], ACT.Tanh, scale=inv_unit[:, t : t + 1])
                for b in range(BLOCKS):
                    cols = slice(b * BLOCK, (b + 1) * BLOCK)
                    nc.tensor.matmul(banks[t][:, cols], emb[:, cols], idents[h][:], start=(b == 0), stop=False, is_transpose=True)
            for b in range(BLOCKS):
                cols = slice(b * BLOCK, (b + 1) * BLOCK)
                gate = sb([P, BLOCK, PACK], F32, "gate%d" % len(gates))
                nc.scalar.activation(gate[:], squashed[:, :, cols].rearrange("p t r -> p r t"), ACT.Exp, scale=0.7)
                gates.append(gate)

            backs = [psum.tile([P, HALF], F32, name="back", tag=("back", "acc")[h], bufs=BANKS)[:] for b in range(BLOCKS)]
            turned = []
            for t in range(PACK):
                hashed = sb([P, HALF], F32, "hashed%d_%d" % (h, t))
                nc.vector.tensor_tensor(hashed[:], mix_win[t][:].indirect(re_sb[:, part]), imp_sb[h][:, t, :], ALU.mult)
                for b in range(BLOCKS):
                    cols = slice(b * BLOCK, (b + 1) * BLOCK)
                    nc.tensor.matmul(
                        banks[t][:, cols], hashed[:, cols], idents[h][:], start=False, stop=(b == BLOCKS - 1), is_transpose=True
                    )
                buf = sb([P, HALF], F32, "turned%d_%d" % (h, t))
                nc.scalar.copy(buf[:], banks[t][:])
                turned.append(buf)
                for b in range(BLOCKS):
                    for u in range(PACK):
                        if (max(b, u) if h == 1 else u) == t:
                            nc.tensor.transpose(
                                backs[b][:, u * BLOCK : (u + 1) * BLOCK], turned[u][:, b * BLOCK : (b + 1) * BLOCK], ident[:]
                            )
            sums.extend(backs)
            if h == 0:
                late_ident = sb([P, P], F32, "late_ident", "hashed0_%d" % (PACK - 1))
                nc.scalar.copy(late_ident[:], ident[:])
                idents.append(late_ident)

        after_gathers = {0: "mix2", OUT_WIDTHS[0]: "mix1"}
        groups = []
        first = 0
        for width in OUT_WIDTHS:
            hid = sb([P, width, PACK], BF16, "hid%d" % first, after_gathers.get(first, ""))
            for r0 in range(first, first + width, BLOCK):
                nc.vector.tensor_tensor(
                    hid[:, r0 - first : r0 - first + BLOCK, :],
                    sums[r0 // BLOCK].rearrange("p (t r) -> p r t", t=PACK),
                    gates[r0 // BLOCK][:],
                    ALU.mult,
                )
            groups.append((hid, first, width))
            first = first + width

        for hid, first, width in groups:
            hq = quantize(hid[:].rearrange("p r t -> p (r t)"), width, "hid%d" % first)
            res = psum.tile([P, width], F32, name="res", tag="acc" if first < HALF else "back", bufs=BANKS)
            product(res[:], w3q, slice(0, N), hq, slice(0, width))
            res_sb = sb([P, width], F32, "res%d" % first)
            copy_out = nc.vector.tensor_copy if width == BLOCK else nc.scalar.copy
            copy_out(res_sb[:], res[:])
            nc.sync.dma_start(out[:, first : first + width], res_sb[:])
